import numpy as np
import ml_dtypes


def mxq(x, axis, fmt="e4m3"):
    dtype, down = {"e4m3": (ml_dtypes.float8_e4m3fn, 7), "e5m2": (ml_dtypes.float8_e5m2, 14)}[fmt]
    v = np.moveaxis(np.asarray(x, np.float32).astype(ml_dtypes.bfloat16).astype(np.float64), axis, -1)
    blocks = v.reshape(v.shape[:-1] + (-1, 32))
    amax = np.abs(blocks).max(-1, keepdims=True)
    byte = np.maximum(np.where(amax > 0, np.frexp(amax)[1] - 1 + 127, 0) - down, 1)
    scale = np.exp2(byte - 127.0)
    codes = (blocks / scale).astype(np.float32).astype(dtype).astype(np.float64)
    return np.moveaxis((codes * scale).reshape(v.shape), -1, axis)


WIDE = False


def mx_kscale(k):
    if not WIDE:
        return np.ones(k)
    levels = np.array([30, -30])
    if k % 512:
        return np.exp2(np.random.permutation(np.resize(levels, k // 32))).repeat(32)
    a = np.empty((k // 512, 16))
    for p in range(k // 512):
        a[p, :8] = np.random.permutation(np.resize(levels, 8))
        for g in range(8):
            far = levels[np.abs(levels - a[p, g]) >= 10]
            a[p, g + 8] = far[np.random.randint(len(far))]
    return np.exp2(a.ravel()).repeat(32)


def f64(x):
    return np.asarray(x).astype(np.float64)


def striped(idx):
    return np.tile(np.asarray(idx).reshape(-1, 16).T, (8, 1)).astype(np.uint16)


def unstriped(offs):
    return offs[:16].T.reshape(-1).astype(np.int64)


E2M1 = np.array([0.0, 0.5, 1.0, 1.5, 2.0, 3.0, 4.0, 6.0, -0.0, -0.5, -1.0, -1.5, -2.0, -3.0, -4.0, -6.0])


def pack_weight(w, fmt):
    k, n = w.shape
    w = f64(np.asarray(w, np.float32).astype(ml_dtypes.bfloat16)).reshape(k // 32, 32, n)
    amax = np.abs(w).max(1)
    if fmt in ("e4m3", "e5m2"):
        byte = np.frexp(amax)[1] - 1 + 127 - (7 if fmt == "e4m3" else 14)
    else:
        mant, ex = np.frexp(amax / 6.0)
        byte = np.where(mant > 0.5, ex, ex - 1) + 127
    byte = np.clip(np.where(amax > 0, byte, 1), 1, 254)
    scaled = (w * np.exp2(127.0 - byte)[:, None, :]).reshape(k, n).astype(np.float32)
    by_word = np.ascontiguousarray(scaled.reshape(k // 512, 128, 4, n).transpose(0, 1, 3, 2))
    if fmt in ("e4m3", "e5m2"):
        words = by_word.astype(ml_dtypes.float8_e4m3fn if fmt == "e4m3" else ml_dtypes.float8_e5m2).view(np.uint8)
    else:
        c = by_word.astype(ml_dtypes.float4_e2m1fn).view(np.uint8) & 0xF
        words = (c[..., 0::2] | (c[..., 1::2] << 4)).reshape(k // 512, 128, 2 * n)
    return np.ascontiguousarray(words), np.ascontiguousarray(byte.astype(np.uint8).reshape(k // 512, 16, n))


def unpack_weight(words, scales, fmt):
    g, _, n = scales.shape
    words = np.ascontiguousarray(words).reshape(g, 128, n, -1)
    if fmt in ("e4m3", "e5m2"):
        vals = words.view(ml_dtypes.float8_e4m3fn if fmt == "e4m3" else ml_dtypes.float8_e5m2).astype(np.float64)
    else:
        nib = np.empty((g, 128, n, 4), np.uint8)
        nib[..., 0::2] = words & 0xF
        nib[..., 1::2] = words >> 4
        vals = E2M1[nib]
    vals = vals * np.repeat(np.exp2(scales.astype(np.float64) - 127.0), 8, axis=1)[..., None]
    return vals.transpose(0, 1, 3, 2).reshape(g * 512, n)


K, T, Z, J, R, C, O, N, E = 512, 1024, 1024, 256, 512, 512, 256, 256, 1024


def setup_inputs():
    n = np.random.standard_normal
    idx = np.random.permutation(T)[:J]
    idx2 = np.random.permutation(Z)[:J]
    idx3 = np.random.permutation(C)[:J]
    idx4 = np.random.permutation(C)[:J]
    idx5 = np.random.permutation(C)[:O]
    idx6 = np.random.permutation(E)[:O]
    fk = mx_kscale(K)
    fr = mx_kscale(R)
    xtp = pack_weight(n((K, T)) / fk[:, None], "e2m1")
    xop = pack_weight(n((K, Z)) / fk[:, None], "e5m2")
    wp = pack_weight(n((K, R)) * 1 / np.sqrt(K) * fk[:, None] * fr, "e5m2")
    wbp = pack_weight(n((R, N)) * 1 / np.sqrt(R) / fr[:, None], "e4m3")
    return {
        "xt_words": xtp[0],
        "xt_scales": xtp[1],
        "xo_words": xop[0],
        "xo_scales": xop[1],
        "w_words": wp[0],
        "w_scales": wp[1],
        "wb_words": wbp[0],
        "wb_scales": wbp[1],
        "tz": (n((N, E))).astype(np.float32),
        "offs": striped(idx),
        "offs2": striped(idx2),
        "offs3": striped(idx3),
        "offs4": striped(idx4),
        "offs5": striped(idx5),
        "offs6": striped(idx6),
    }


def reference(xt_words, xt_scales, xo_words, xo_scales, w_words, w_scales, wb_words, wb_scales, tz, offs, offs2, offs3, offs4, offs5, offs6):
    idx = unstriped(offs)
    idx2 = unstriped(offs2)
    idx3 = unstriped(offs3)
    idx4 = unstriped(offs4)
    idx5 = unstriped(offs5)
    idx6 = unstriped(offs6)
    xtu = unpack_weight(xt_words, xt_scales, "e2m1")
    xou = unpack_weight(xo_words, xo_scales, "e5m2")
    wu = unpack_weight(w_words, w_scales, "e5m2")
    wbu = unpack_weight(wb_words, wb_scales, "e4m3")
    xtidxg = xtu[:, idx]
    a = wu.T @ xtidxg
    xoidx2g = xou[:, idx2]
    b = wu.T @ xoidx2g
    pw = np.zeros((R, C))
    pw[:, idx3] = a
    pv = np.zeros((R, C))
    pv[:, idx4] = b
    pg = pw + pv
    hid = pg[:, idx5]
    hidq = mxq(hid, 0, "e5m2")
    p = wbu.T @ hidq
    y = p + f64(tz)[:, idx6]
    return y

@@ -1,0 +1,145 @@
+from contextlib import ExitStack
+
+import concourse.mybir as mybir
+
+K, T, Z, J, R, C, O, N, E = 512, 1024, 1024, 256, 512, 512, 256, 256, 1024
+FLOPS = 2 * K * R * J * 2 + 2 * R * N * O
+
+F32 = mybir.dt.float32
+BF16 = mybir.dt.bfloat16
+I32 = mybir.dt.int32
+U32 = mybir.dt.uint32
+U16 = mybir.dt.uint16
+U8 = mybir.dt.uint8
+E2M1 = mybir.dt.float4_e2m1fn_x4
+E5M2 = mybir.dt.float8_e5m2_x4
+E4M3 = mybir.dt.float8_e4m3fn_x4
+COPY = mybir.ActivationFunctionType.Copy
+ADD = mybir.AluOpType.add
+
+P = 128
+PACK = 4
+
+
+def tile_list_oneforboth_shared_one_tabled_kernel(
+    tc, xt_words, xt_scales, xo_words, xo_scales, w_words, w_scales, wb_words, wb_scales,
+    tz, offs, offs2, offs3, offs4, offs5, offs6, out,
+):
+    nc = tc.nc
+    with ExitStack() as ctx:
+        sb = ctx.enter_context(tc.tile_pool(name="sb", bufs=1))
+        ps = ctx.enter_context(tc.psum_pool(name="ps", bufs=1))
+
+        def tile(name, shape, dtype):
+            return sb.tile(shape, dtype, name=name, align_bytes=64)
+
+        def load_list(name, src):
+            t = tile(name, [P, 16], U16)
+            nc.sync.dma_start(t[:], src)
+            return t
+
+        def zero_plane(name, width):
+            t = tile(name, [P, width], U8)
+            nc.vector.memset(t[:].bitcast(I32), 0)
+            return t
+
+        def load_plane(t, src, queue):
+            for q in range(4):
+                queue.dma_start(t[32 * q : 32 * q + 4, :].bitcast(I32), src[0, 4 * q : 4 * q + 4, :].bitcast(I32))
+
+        def load_words(name, src, width, queue):
+            t = tile(name, [P, width], U32)
+            queue.dma_start(t[:].bitcast(I32), src[0].rearrange("p n t -> p (n t)").bitcast(I32))
+            return t
+
+        w_s = zero_plane("w_s", R)
+        xt_s = zero_plane("xt_s", T)
+        xo_s = zero_plane("xo_s", Z)
+        wb_s = zero_plane("wb_s", N)
+
+        w_w = load_words("w_w", w_words, R, nc.sync)
+        load_plane(w_s, w_scales, nc.sync)
+        l1 = load_list("l1", offs)
+        xt_w = tile("xt_w", [P, T], U16)
+        nc.sync.dma_start(xt_w[:].bitcast(I32), xt_words[0].bitcast(I32))
+        load_plane(xt_s, xt_scales, nc.sync)
+        l2 = load_list("l2", offs2)
+        xo_w = load_words("xo_w", xo_words, Z, nc.sync)
+        load_plane(xo_s, xo_scales, nc.sync)
+        l3 = load_list("l3", offs3)
+        l4 = load_list("l4", offs4)
+        l5 = load_list("l5", offs5)
+        l6 = load_list("l6", offs6)
+        tzs = []
+        for h in range(2):
+            t = tile("tz%d" % h, [P, E], F32)
+            nc.sync.dma_start(t[:], tz[P * h : P * (h + 1), :])
+            tzs.append(t)
+        wb_w = load_words("wb_w", wb_words, N, nc.sync)
+        load_plane(wb_s, wb_scales, nc.sync)
+
+        pw = [tile("pw%d" % t, [P, C], F32) for t in range(PACK)]
+        pv = [tile("pv%d" % t, [P, C], F32) for t in range(PACK)]
+        for t in range(PACK):
+            eng = nc.vector if t < 2 else nc.gpsimd
+            eng.memset(pw[t][:], 0.0)
+            eng.memset(pv[t][:], 0.0)
+
+        wp_w = tile("wp_w", [P, PACK, P], U32)
+        wp_s = tile("wp_s", [P, PACK, P], U8)
+        nc.vector.tensor_copy(wp_w[:].bitcast(I32), w_w[:].bitcast(I32).rearrange("p (m t) -> p t m", t=PACK))
+        nc.vector.tensor_copy(wp_s[:], w_s[:].rearrange("p (m t) -> p t m", t=PACK))
+
+        g1_w = tile("g1_w", [P, J], U16)
+        g1_s = tile("g1_s", [P, J], U8)
+        g2_w = tile("g2_w", [P, J], U32)
+        g2_s = tile("g2_s", [P, J], U8)
+        nc.vector.tensor_copy(g1_w[:], xt_w[:].indirect(l1[:]))
+        nc.vector.tensor_copy(g1_s[:], xt_s[:].indirect(l1[:]))
+        nc.vector.tensor_copy(g2_w[:], xo_w[:].indirect(l2[:]))
+        nc.vector.tensor_copy(g2_s[:], xo_s[:].indirect(l2[:]))
+
+        def first(name, t, words, scales):
+            acc = ps.tile([P, J], F32, name=name)
+            nc.tensor.matmul_mx(
+                out=acc[:], lhsT=wp_w[:, t, :].bitcast(E5M2), lhsT_scale=wp_s[:, t, :],
+                rhs=words, rhs_scale=scales, start=True, stop=True,
+            )
+            return acc
+
+        a_ps = [first("a%d" % t, t, g1_w[:].bitcast(E2M1), g1_s[:]) for t in range(PACK)]
+        b_ps = [first("b%d" % t, t, g2_w[:].bitcast(E5M2), g2_s[:]) for t in range(PACK)]
+
+        hid = tile("hid", [P, O, PACK], BF16)
+        for t in range(PACK):
+            a_sb = tile("a_sb%d" % t, [P, J], F32)
+            b_sb = tile("b_sb%d" % t, [P, J], F32)
+            nc.scalar.copy(a_sb[:], a_ps[t][:])
+            if t == 0:
+                nc.vector.tensor_copy(b_sb[:], b_ps[t][:])
+            else:
+                nc.scalar.copy(b_sb[:], b_ps[t][:])
+            nc.scalar.activation(pw[t][:].indirect(l3[:]), a_sb[:], COPY)
+            if t < 3:
+                nc.vector.tensor_copy(pv[t][:].indirect(l4[:]), b_sb[:])
+            else:
+                nc.scalar.activation(pv[t][:].indirect(l4[:]), b_sb[:], COPY)
+            pg = tile("pg%d" % t, [P, C], F32)
+            nc.vector.tensor_tensor(pg[:], pw[t][:], pv[t][:], ADD)
+            nc.vector.tensor_copy(hid[:, :, t], pg[:].indirect(l5[:]))
+
+        h_w = tile("h_w", [P, O], U32)
+        h_s = tile("h_s", [P, O], U8)
+        nc.vector.quantize_mx(out=h_w[:].bitcast(E5M2), scales=h_s[:], in_=hid[:].rearrange("p o t -> p (o t)"))
+
+        for h in range(2):
+            tg = tile("tg%d" % h, [P, O], F32)
+            nc.scalar.activation(tg[:], tzs[h][:].indirect(l6[:]), COPY)
+            acc = ps.tile([P, O], F32, name="a%d" % h)
+            nc.tensor.matmul_mx(
+                out=acc[:], lhsT=wb_w[:, P * h : P * (h + 1)].bitcast(E4M3), lhsT_scale=wb_s[:, P * h : P * (h + 1)],
+                rhs=h_w[:].bitcast(E5M2), rhs_scale=h_s[:], start=True, stop=True,
+            )
+            y = tile("y%d" % h, [P, O], F32)
+            nc.vector.tensor_tensor(y[:], acc[:], tg[:], ADD)
+            nc.sync.dma_start(out[P * h : P * (h + 1), :], y[:])

@@ -30,39 +30,39 @@ def tile_list_oneforboth_shared_one_tabled_kernel(
         sb = ctx.enter_context(tc.tile_pool(name="sb", bufs=1))
         ps = ctx.enter_context(tc.psum_pool(name="ps", bufs=1))
 
-        def tile(name, shape, dtype):
-            return sb.tile(shape, dtype, name=name, align_bytes=64)
+        def tile(name, shape, dtype, tag=None):
+            return sb.tile(shape, dtype, name=name, tag=tag or name, align_bytes=64)
 
         def load_list(name, src):
             t = tile(name, [P, 16], U16)
             nc.sync.dma_start(t[:], src)
             return t
 
-        def zero_plane(name, width):
-            t = tile(name, [P, width], U8)
-            nc.vector.memset(t[:].bitcast(I32), 0)
+        def zero_plane(name, width, eng, tag=None):
+            t = tile(name, [P, width], U8, tag)
+            eng.memset(t[:].bitcast(I32), 0)
             return t
 
         def load_plane(t, src, queue):
             for q in range(4):
                 queue.dma_start(t[32 * q : 32 * q + 4, :].bitcast(I32), src[0, 4 * q : 4 * q + 4, :].bitcast(I32))
 
-        def load_words(name, src, width, queue):
-            t = tile(name, [P, width], U32)
+        def load_words(name, src, width, queue, tag=None):
+            t = tile(name, [P, width], U32, tag)
             queue.dma_start(t[:].bitcast(I32), src[0].rearrange("p n t -> p (n t)").bitcast(I32))
             return t
 
-        w_s = zero_plane("w_s", R)
-        xt_s = zero_plane("xt_s", T)
-        xo_s = zero_plane("xo_s", Z)
-        wb_s = zero_plane("wb_s", N)
+        xt_s = zero_plane("xt_s", T, nc.gpsimd)
+        w_s = zero_plane("w_s", R, nc.vector)
+        xo_s = zero_plane("xo_s", Z, nc.gpsimd)
 
+        load_plane(xt_s, xt_scales, nc.sync)
+        w_land = tile("w_land", [4, 4, R], U8)
+        nc.sync.dma_start(w_land[:].bitcast(I32), w_scales[0].bitcast(I32).rearrange("(q r) n -> r q n", r=4))
         w_w = load_words("w_w", w_words, R, nc.sync)
-        load_plane(w_s, w_scales, nc.sync)
         l1 = load_list("l1", offs)
         xt_w = tile("xt_w", [P, T], U16)
         nc.sync.dma_start(xt_w[:].bitcast(I32), xt_words[0].bitcast(I32))
-        load_plane(xt_s, xt_scales, nc.sync)
         l2 = load_list("l2", offs2)
         xo_w = load_words("xo_w", xo_words, Z, nc.sync)
         load_plane(xo_s, xo_scales, nc.sync)
@@ -70,76 +70,112 @@ def tile_list_oneforboth_shared_one_tabled_kernel(
         l4 = load_list("l4", offs4)
         l5 = load_list("l5", offs5)
         l6 = load_list("l6", offs6)
-        tzs = []
-        for h in range(2):
-            t = tile("tz%d" % h, [P, E], F32)
-            nc.sync.dma_start(t[:], tz[P * h : P * (h + 1), :])
-            tzs.append(t)
-        wb_w = load_words("wb_w", wb_words, N, nc.sync)
-        load_plane(wb_s, wb_scales, nc.sync)
 
-        pw = [tile("pw%d" % t, [P, C], F32) for t in range(PACK)]
-        pv = [tile("pv%d" % t, [P, C], F32) for t in range(PACK)]
-        for t in range(PACK):
-            eng = nc.vector if t < 2 else nc.gpsimd
-            eng.memset(pw[t][:], 0.0)
-            eng.memset(pv[t][:], 0.0)
+        pw = [tile("pw%d" % t, [P, C], F32) for t in range(2)]
+        for t in range(2):
+            nc.vector.memset(pw[t][:], 0.0)
 
+        for q in range(4):
+            nc.vector.tensor_copy(w_s[32 * q : 32 * q + 4, :].bitcast(I32), w_land[:, q, :].bitcast(I32))
         wp_w = tile("wp_w", [P, PACK, P], U32)
         wp_s = tile("wp_s", [P, PACK, P], U8)
-        nc.vector.tensor_copy(wp_w[:].bitcast(I32), w_w[:].bitcast(I32).rearrange("p (m t) -> p t m", t=PACK))
+        nc.scalar.copy(wp_w[:], w_w[:].rearrange("p (m t) -> p t m", t=PACK))
         nc.vector.tensor_copy(wp_s[:], w_s[:].rearrange("p (m t) -> p t m", t=PACK))
 
         g1_w = tile("g1_w", [P, J], U16)
         g1_s = tile("g1_s", [P, J], U8)
         g2_w = tile("g2_w", [P, J], U32)
         g2_s = tile("g2_s", [P, J], U8)
-        nc.vector.tensor_copy(g1_w[:], xt_w[:].indirect(l1[:]))
         nc.vector.tensor_copy(g1_s[:], xt_s[:].indirect(l1[:]))
+        nc.vector.tensor_copy(g1_w[:], xt_w[:].indirect(l1[:]))
         nc.vector.tensor_copy(g2_w[:], xo_w[:].indirect(l2[:]))
         nc.vector.tensor_copy(g2_s[:], xo_s[:].indirect(l2[:]))
 
-        def first(name, t, words, scales):
-            acc = ps.tile([P, J], F32, name=name)
-            nc.tensor.matmul_mx(
-                out=acc[:], lhsT=wp_w[:, t, :].bitcast(E5M2), lhsT_scale=wp_s[:, t, :],
-                rhs=words, rhs_scale=scales, start=True, stop=True,
-            )
+
+        def first(name, slices, words, scales):
+            acc = ps.tile([P, len(slices), J], F32, name=name)
+            for i, t in enumerate(slices):
+                nc.tensor.matmul_mx(
+                    out=acc[:, i, :], lhsT=wp_w[:, t, :].bitcast(E5M2), lhsT_scale=wp_s[:, t, :],
+                    rhs=words, rhs_scale=scales, start=True, stop=True,
+                )
             return acc
 
-        a_ps = [first("a%d" % t, t, g1_w[:].bitcast(E2M1), g1_s[:]) for t in range(PACK)]
-        b_ps = [first("b%d" % t, t, g2_w[:].bitcast(E5M2), g2_s[:]) for t in range(PACK)]
+        a_ps = [first("a%d" % u, s, g1_w[:].bitcast(E2M1), g1_s[:]) for u, s in enumerate(((0,), (1,), (2, 3)))]
+        b_ps = [first("b%d" % u, s, g2_w[:].bitcast(E5M2), g2_s[:]) for u, s in enumerate(((0, 1), (2,), (3,)))]
+        a_first = tile("a_first", [P, 1, J], F32)
+        a_rest = tile("a_rest", [P, 3, J], F32, "xo_s")
+        a_sb = [a_first[:], a_rest[:, 0:1, :], a_rest[:, 1:3, :]]
+        b_sb = [tile("b_sb%d" % u, [P, n, J], F32) for u, n in enumerate((2, 1, 1))]
+        a = [a_first[:, 0, :]] + [a_rest[:, i, :] for i in range(3)]
+        b = [b_sb[0][:, 0, :], b_sb[0][:, 1, :], b_sb[1][:, 0, :], b_sb[2][:, 0, :]]
+        pv = [tile("pv%d" % t, [P, C], F32, tag) for t, tag in enumerate(("w_w", "w_s", "xt_w", "g1_w"))]
+        pw = pw + [tile("pw%d" % t, [P, C], F32, tag) for t, tag in ((2, "xt_s"), (3, "xo_w"))]
+        for board in (pv[1], pv[0], pw[2], pv[2], pw[3], pv[3]):
+            nc.gpsimd.memset(board[:], 0.0)
+        tzs = tile("tz", [P, 2, E], F32, "w_land")
+        nc.sync.dma_start(tzs[:], tz.rearrange("(h p) e -> p h e", p=P))
+        wb_s = zero_plane("wb_s", N, nc.gpsimd, "g1_s")
+        load_plane(wb_s, wb_scales, nc.sync)
+        wb_w = load_words("wb_w", wb_words, N, nc.sync, "wp_w")
+        pg = {}
+        hid = tile("hid", [P, O, PACK], BF16, "b_sb1")
 
-        hid = tile("hid", [P, O, PACK], BF16)
-        for t in range(PACK):
-            a_sb = tile("a_sb%d" % t, [P, J], F32)
-            b_sb = tile("b_sb%d" % t, [P, J], F32)
-            nc.scalar.copy(a_sb[:], a_ps[t][:])
-            if t == 0:
-                nc.vector.tensor_copy(b_sb[:], b_ps[t][:])
+        def evac(eng, dst, src):
+            if eng == "s":
+                nc.scalar.copy(dst, src[:])
             else:
-                nc.scalar.copy(b_sb[:], b_ps[t][:])
-            nc.scalar.activation(pw[t][:].indirect(l3[:]), a_sb[:], COPY)
-            if t < 3:
-                nc.vector.tensor_copy(pv[t][:].indirect(l4[:]), b_sb[:])
+                nc.vector.tensor_copy(dst, src[:])
+
+        def put(eng, board, lst, src, t):
+            if eng == "s":
+                nc.scalar.activation(board[t][:].indirect(lst[:]), src[t], COPY)
             else:
-                nc.scalar.activation(pv[t][:].indirect(l4[:]), b_sb[:], COPY)
-            pg = tile("pg%d" % t, [P, C], F32)
-            nc.vector.tensor_tensor(pg[:], pw[t][:], pv[t][:], ADD)
-            nc.vector.tensor_copy(hid[:, :, t], pg[:].indirect(l5[:]))
+                nc.vector.tensor_copy(board[t][:].indirect(lst[:]), src[t])
+
+        def join(eng, t):
+            pg[t] = tile("pg%d" % t, [P, C], F32, "pg%d" % min(t, 2))
+            eng.tensor_tensor(pg[t][:], pw[t][:], pv[t][:], ADD)
+
+        def read(t):
+            nc.vector.tensor_copy(hid[:, :, t], pg[t][:].indirect(l5[:]))
+
+        evac("s", a_sb[0], a_ps[0])
+        put("s", pw, l3, a, 0)
+        evac("v", a_sb[1], a_ps[1])
+        put("v", pw, l3, a, 1)
+        evac("s", b_sb[0][:], b_ps[0])
+        evac("v", a_sb[2], a_ps[2])
+        put("s", pv, l4, b, 1)
+        put("v", pv, l4, b, 0)
+        join(nc.gpsimd, 1)
+        join(nc.gpsimd, 0)
+        evac("v", b_sb[1][:], b_ps[1])
+        put("s", pw, l3, a, 2)
+        put("v", pv, l4, b, 2)
+        join(nc.gpsimd, 2)
+        evac("s", b_sb[2][:], b_ps[2])
+        put("s", pw, l3, a, 3)
+        put("s", pv, l4, b, 3)
+        read(1)
+        read(0)
+        read(2)
+        join(nc.vector, 3)
+        read(3)
 
         h_w = tile("h_w", [P, O], U32)
         h_s = tile("h_s", [P, O], U8)
         nc.vector.quantize_mx(out=h_w[:].bitcast(E5M2), scales=h_s[:], in_=hid[:].rearrange("p o t -> p (o t)"))
 
+        tg = tile("tg", [P, 2, O], F32, "b_sb2")
         for h in range(2):
-            tg = tile("tg%d" % h, [P, O], F32)
-            nc.scalar.activation(tg[:], tzs[h][:].indirect(l6[:]), COPY)
-            acc = ps.tile([P, O], F32, name="a%d" % h)
+            nc.scalar.activation(tg[:, h, :], tzs[:, h, :].indirect(l6[:]), COPY)
+        for h, queue in enumerate((nc.sync, nc.scalar)):
+            acc = ps.tile([P, O], F32, name="p%d" % h)
             nc.tensor.matmul_mx(
                 out=acc[:], lhsT=wb_w[:, P * h : P * (h + 1)].bitcast(E4M3), lhsT_scale=wb_s[:, P * h : P * (h + 1)],
                 rhs=h_w[:].bitcast(E5M2), rhs_scale=h_s[:], start=True, stop=True,
             )
             y = tile("y%d" % h, [P, O], F32)
-            nc.vector.tensor_tensor(y[:], acc[:], tg[:], ADD)
-            nc.sync.dma_start(out[P * h : P * (h + 1), :], y[:])
+            nc.vector.tensor_tensor(y[:], acc[:], tg[:, h, :], ADD)
+            queue.dma_start(out[P * h : P * (h + 1), :], y[:])

@@ -59,12 +59,12 @@ def tile_list_oneforboth_shared_one_tabled_kernel(
         load_plane(xt_s, xt_scales, nc.sync)
         w_land = tile("w_land", [4, 4, R], U8)
         nc.sync.dma_start(w_land[:].bitcast(I32), w_scales[0].bitcast(I32).rearrange("(q r) n -> r q n", r=4))
-        w_w = load_words("w_w", w_words, R, nc.sync)
         l1 = load_list("l1", offs)
+        w_w = load_words("w_w", w_words, R, nc.sync)
         xt_w = tile("xt_w", [P, T], U16)
         nc.sync.dma_start(xt_w[:].bitcast(I32), xt_words[0].bitcast(I32))
-        l2 = load_list("l2", offs2)
         xo_w = load_words("xo_w", xo_words, Z, nc.sync)
+        l2 = load_list("l2", offs2)
         load_plane(xo_s, xo_scales, nc.sync)
         l3 = load_list("l3", offs3)
         l4 = load_list("l4", offs4)
@@ -80,7 +80,8 @@ def tile_list_oneforboth_shared_one_tabled_kernel(
         wp_w = tile("wp_w", [P, PACK, P], U32)
         wp_s = tile("wp_s", [P, PACK, P], U8)
         nc.scalar.copy(wp_w[:], w_w[:].rearrange("p (m t) -> p t m", t=PACK))
-        nc.vector.tensor_copy(wp_s[:], w_s[:].rearrange("p (m t) -> p t m", t=PACK))
+        for u in range(2):
+            nc.gpsimd.tensor_copy(wp_s[:, 2 * u : 2 * u + 2, :], w_s[:].rearrange("p (m t) -> p t m", t=PACK)[:, 2 * u : 2 * u + 2, :])
 
         g1_w = tile("g1_w", [P, J], U16)
         g1_s = tile("g1_s", [P, J], U8)
@@ -110,8 +111,8 @@ def tile_list_oneforboth_shared_one_tabled_kernel(
         a = [a_first[:, 0, :]] + [a_rest[:, i, :] for i in range(3)]
         b = [b_sb[0][:, 0, :], b_sb[0][:, 1, :], b_sb[1][:, 0, :], b_sb[2][:, 0, :]]
         pv = [tile("pv%d" % t, [P, C], F32, tag) for t, tag in enumerate(("w_w", "w_s", "xt_w", "g1_w"))]
-        pw = pw + [tile("pw%d" % t, [P, C], F32, tag) for t, tag in ((2, "xt_s"), (3, "xo_w"))]
-        for board in (pv[1], pv[0], pw[2], pv[2], pw[3], pv[3]):
+        pw = pw + [tile("pw%d" % t, [P, C], F32, tag) for t, tag in ((2, "g2_w"), (3, "g2_s"))]
+        for board in (pv[1], pv[0], pv[2], pv[3], pw[2], pw[3]):
             nc.gpsimd.memset(board[:], 0.0)
         tzs = tile("tz", [P, 2, E], F32, "w_land")
         nc.sync.dma_start(tzs[:], tz.rearrange("(h p) e -> p h e", p=P))
@@ -147,14 +148,14 @@ def tile_list_oneforboth_shared_one_tabled_kernel(
         evac("s", b_sb[0][:], b_ps[0])
         evac("v", a_sb[2], a_ps[2])
         put("s", pv, l4, b, 1)
+        evac("v", b_sb[1][:], b_ps[1])
         put("v", pv, l4, b, 0)
         join(nc.gpsimd, 1)
         join(nc.gpsimd, 0)
-        evac("v", b_sb[1][:], b_ps[1])
         put("s", pw, l3, a, 2)
         put("v", pv, l4, b, 2)
         join(nc.gpsimd, 2)
-        evac("s", b_sb[2][:], b_ps[2])
+        evac("v", b_sb[2][:], b_ps[2])
         put("s", pw, l3, a, 3)
         put("s", pv, l4, b, 3)
         read(1)

from contextlib import ExitStack

import concourse.mybir as mybir

K, T, Z, J, R, C, O, N, E = 512, 1024, 1024, 256, 512, 512, 256, 256, 1024
FLOPS = 2 * K * R * J * 2 + 2 * R * N * O

F32 = mybir.dt.float32
BF16 = mybir.dt.bfloat16
I32 = mybir.dt.int32
U32 = mybir.dt.uint32
U16 = mybir.dt.uint16
U8 = mybir.dt.uint8
E2M1 = mybir.dt.float4_e2m1fn_x4
E5M2 = mybir.dt.float8_e5m2_x4
E4M3 = mybir.dt.float8_e4m3fn_x4
COPY = mybir.ActivationFunctionType.Copy
ADD = mybir.AluOpType.add

P = 128
PACK = 4


def tile_list_oneforboth_shared_one_tabled_kernel(
    tc, xt_words, xt_scales, xo_words, xo_scales, w_words, w_scales, wb_words, wb_scales,
    tz, offs, offs2, offs3, offs4, offs5, offs6, out,
):
    nc = tc.nc
    with ExitStack() as ctx:
        sb = ctx.enter_context(tc.tile_pool(name="sb", bufs=1))
        ps = ctx.enter_context(tc.psum_pool(name="ps", bufs=1))

        def tile(name, shape, dtype, tag=None):
            return sb.tile(shape, dtype, name=name, tag=tag or name, align_bytes=64)

        def load_list(name, src):
            t = tile(name, [P, 16], U16)
            nc.sync.dma_start(t[:], src)
            return t

        def zero_plane(name, width, eng, tag=None):
            t = tile(name, [P, width], U8, tag)
            eng.memset(t[:].bitcast(I32), 0)
            return t

        def load_plane(t, src, queue):
            for q in range(4):
                queue.dma_start(t[32 * q : 32 * q + 4, :].bitcast(I32), src[0, 4 * q : 4 * q + 4, :].bitcast(I32))

        def load_words(name, src, width, queue, tag=None):
            t = tile(name, [P, width], U32, tag)
            queue.dma_start(t[:].bitcast(I32), src[0].rearrange("p n t -> p (n t)").bitcast(I32))
            return t

        xt_s = zero_plane("xt_s", T, nc.gpsimd)
        w_s = zero_plane("w_s", R, nc.vector)
        xo_s = zero_plane("xo_s", Z, nc.gpsimd)

        load_plane(xt_s, xt_scales, nc.sync)
        w_land = tile("w_land", [4, 4, R], U8)
        nc.sync.dma_start(w_land[:].bitcast(I32), w_scales[0].bitcast(I32).rearrange("(q r) n -> r q n", r=4))
        l1 = load_list("l1", offs)
        w_w = load_words("w_w", w_words, R, nc.sync)
        xt_w = tile("xt_w", [P, T], U16)
        nc.sync.dma_start(xt_w[:].bitcast(I32), xt_words[0].bitcast(I32))
        xo_w = load_words("xo_w", xo_words, Z, nc.sync)
        l2 = load_list("l2", offs2)
        load_plane(xo_s, xo_scales, nc.sync)
        l3 = load_list("l3", offs3)
        l4 = load_list("l4", offs4)
        l5 = load_list("l5", offs5)
        l6 = load_list("l6", offs6)

        pw = [tile("pw%d" % t, [P, C], F32) for t in range(2)]
        for t in range(2):
            nc.vector.memset(pw[t][:], 0.0)

        for q in range(4):
            nc.vector.tensor_copy(w_s[32 * q : 32 * q + 4, :].bitcast(I32), w_land[:, q, :].bitcast(I32))
        wp_w = tile("wp_w", [P, PACK, P], U32)
        wp_s = tile("wp_s", [P, PACK, P], U8)
        nc.scalar.copy(wp_w[:], w_w[:].rearrange("p (m t) -> p t m", t=PACK))
        for u in range(2):
            nc.gpsimd.tensor_copy(wp_s[:, 2 * u : 2 * u + 2, :], w_s[:].rearrange("p (m t) -> p t m", t=PACK)[:, 2 * u : 2 * u + 2, :])

        g1_w = tile("g1_w", [P, J], U16)
        g1_s = tile("g1_s", [P, J], U8)
        g2_w = tile("g2_w", [P, J], U32)
        g2_s = tile("g2_s", [P, J], U8)
        nc.vector.tensor_copy(g1_s[:], xt_s[:].indirect(l1[:]))
        nc.vector.tensor_copy(g1_w[:], xt_w[:].indirect(l1[:]))
        nc.vector.tensor_copy(g2_w[:], xo_w[:].indirect(l2[:]))
        nc.vector.tensor_copy(g2_s[:], xo_s[:].indirect(l2[:]))


        def first(name, slices, words, scales):
            acc = ps.tile([P, len(slices), J], F32, name=name)
            for i, t in enumerate(slices):
                nc.tensor.matmul_mx(
                    out=acc[:, i, :], lhsT=wp_w[:, t, :].bitcast(E5M2), lhsT_scale=wp_s[:, t, :],
                    rhs=words, rhs_scale=scales, start=True, stop=True,
                )
            return acc

        a_ps = [first("a%d" % u, s, g1_w[:].bitcast(E2M1), g1_s[:]) for u, s in enumerate(((0,), (1,), (2, 3)))]
        b_ps = [first("b%d" % u, s, g2_w[:].bitcast(E5M2), g2_s[:]) for u, s in enumerate(((0, 1), (2,), (3,)))]
        a_first = tile("a_first", [P, 1, J], F32)
        a_rest = tile("a_rest", [P, 3, J], F32, "xo_s")
        a_sb = [a_first[:], a_rest[:, 0:1, :], a_rest[:, 1:3, :]]
        b_sb = [tile("b_sb%d" % u, [P, n, J], F32) for u, n in enumerate((2, 1, 1))]
        a = [a_first[:, 0, :]] + [a_rest[:, i, :] for i in range(3)]
        b = [b_sb[0][:, 0, :], b_sb[0][:, 1, :], b_sb[1][:, 0, :], b_sb[2][:, 0, :]]
        pv = [tile("pv%d" % t, [P, C], F32, tag) for t, tag in enumerate(("w_w", "w_s", "xt_w", "g1_w"))]
        pw = pw + [tile("pw%d" % t, [P, C], F32, tag) for t, tag in ((2, "g2_w"), (3, "g2_s"))]
        for board in (pv[1], pv[0], pv[2], pv[3], pw[2], pw[3]):
            nc.gpsimd.memset(board[:], 0.0)
        tzs = tile("tz", [P, 2, E], F32, "w_land")
        nc.sync.dma_start(tzs[:], tz.rearrange("(h p) e -> p h e", p=P))
        wb_s = zero_plane("wb_s", N, nc.gpsimd, "g1_s")
        load_plane(wb_s, wb_scales, nc.sync)
        wb_w = load_words("wb_w", wb_words, N, nc.sync, "wp_w")
        pg = {}
        hid = tile("hid", [P, O, PACK], BF16, "b_sb1")

        def evac(eng, dst, src):
            if eng == "s":
                nc.scalar.copy(dst, src[:])
            else:
                nc.vector.tensor_copy(dst, src[:])

        def put(eng, board, lst, src, t):
            if eng == "s":
                nc.scalar.activation(board[t][:].indirect(lst[:]), src[t], COPY)
            else:
                nc.vector.tensor_copy(board[t][:].indirect(lst[:]), src[t])

        def join(eng, t):
            pg[t] = tile("pg%d" % t, [P, C], F32, "pg%d" % min(t, 2))
            eng.tensor_tensor(pg[t][:], pw[t][:], pv[t][:], ADD)

        def read(t):
            nc.vector.tensor_copy(hid[:, :, t], pg[t][:].indirect(l5[:]))

        evac("s", a_sb[0], a_ps[0])
        put("s", pw, l3, a, 0)
        evac("v", a_sb[1], a_ps[1])
        put("v", pw, l3, a, 1)
        evac("s", b_sb[0][:], b_ps[0])
        evac("v", a_sb[2], a_ps[2])
        put("s", pv, l4, b, 1)
        evac("v", b_sb[1][:], b_ps[1])
        put("v", pv, l4, b, 0)
        join(nc.gpsimd, 1)
        join(nc.gpsimd, 0)
        put("s", pw, l3, a, 2)
        put("v", pv, l4, b, 2)
        join(nc.gpsimd, 2)
        evac("v", b_sb[2][:], b_ps[2])
        put("s", pw, l3, a, 3)
        put("s", pv, l4, b, 3)
        read(1)
        read(0)
        read(2)
        join(nc.vector, 3)
        read(3)

        h_w = tile("h_w", [P, O], U32)
        h_s = tile("h_s", [P, O], U8)
        nc.vector.quantize_mx(out=h_w[:].bitcast(E5M2), scales=h_s[:], in_=hid[:].rearrange("p o t -> p (o t)"))

        tg = tile("tg", [P, 2, O], F32, "b_sb2")
        for h in range(2):
            nc.scalar.activation(tg[:, h, :], tzs[:, h, :].indirect(l6[:]), COPY)
        for h, queue in enumerate((nc.sync, nc.scalar)):
            acc = ps.tile([P, O], F32, name="p%d" % h)
            nc.tensor.matmul_mx(
                out=acc[:], lhsT=wb_w[:, P * h : P * (h + 1)].bitcast(E4M3), lhsT_scale=wb_s[:, P * h : P * (h + 1)],
                rhs=h_w[:].bitcast(E5M2), rhs_scale=h_s[:], start=True, stop=True,
            )
            y = tile("y%d" % h, [P, O], F32)
            nc.vector.tensor_tensor(y[:], acc[:], tg[:, h, :], ADD)
            queue.dma_start(out[P * h : P * (h + 1), :], y[:])
